import numpy as np
import ml_dtypes


def mxq(x, axis, fmt="e4m3"):
    dtype, down = {"e4m3": (ml_dtypes.float8_e4m3fn, 7), "e5m2": (ml_dtypes.float8_e5m2, 14)}[fmt]
    v = np.moveaxis(np.asarray(x, np.float32).astype(ml_dtypes.bfloat16).astype(np.float64), axis, -1)
    blocks = v.reshape(v.shape[:-1] + (-1, 32))
    amax = np.abs(blocks).max(-1, keepdims=True)
    byte = np.maximum(np.where(amax > 0, np.frexp(amax)[1] - 1 + 127, 0) - down, 1)
    scale = np.exp2(byte - 127.0)
    codes = (blocks / scale).astype(np.float32).astype(dtype).astype(np.float64)
    return np.moveaxis((codes * scale).reshape(v.shape), -1, axis)


WIDE = False


def mx_kscale(k):
    if not WIDE:
        return np.ones(k)
    levels = np.array([30, -30])
    if k % 512:
        return np.exp2(np.random.permutation(np.resize(levels, k // 32))).repeat(32)
    a = np.empty((k // 512, 16))
    for p in range(k // 512):
        a[p, :8] = np.random.permutation(np.resize(levels, 8))
        for g in range(8):
            far = levels[np.abs(levels - a[p, g]) >= 10]
            a[p, g + 8] = far[np.random.randint(len(far))]
    return np.exp2(a.ravel()).repeat(32)


def f64(x):
    return np.asarray(x).astype(np.float64)


def striped(idx):
    return np.tile(np.asarray(idx).reshape(-1, 16).T, (8, 1)).astype(np.uint16)


def unstriped(offs):
    return offs[:16].T.reshape(-1).astype(np.int64)


E2M1 = np.array([0.0, 0.5, 1.0, 1.5, 2.0, 3.0, 4.0, 6.0, -0.0, -0.5, -1.0, -1.5, -2.0, -3.0, -4.0, -6.0])


def pack_weight(w, fmt):
    k, n = w.shape
    w = f64(np.asarray(w, np.float32).astype(ml_dtypes.bfloat16)).reshape(k // 32, 32, n)
    amax = np.abs(w).max(1)
    if fmt == "e4m3":
        byte = np.frexp(amax)[1] - 1 + 127 - 7
    else:
        mant, ex = np.frexp(amax / 6.0)
        byte = np.where(mant > 0.5, ex, ex - 1) + 127
    byte = np.clip(np.where(amax > 0, byte, 1), 1, 254)
    scaled = (w * np.exp2(127.0 - byte)[:, None, :]).reshape(k, n).astype(np.float32)
    by_word = np.ascontiguousarray(scaled.reshape(k // 512, 128, 4, n).transpose(0, 1, 3, 2))
    if fmt == "e4m3":
        words = by_word.astype(ml_dtypes.float8_e4m3fn).view(np.uint8)
    else:
        c = by_word.astype(ml_dtypes.float4_e2m1fn).view(np.uint8) & 0xF
        words = (c[..., 0::2] | (c[..., 1::2] << 4)).reshape(k // 512, 128, 2 * n)
    return np.ascontiguousarray(words), np.ascontiguousarray(byte.astype(np.uint8).reshape(k // 512, 16, n))


def unpack_weight(words, scales, fmt):
    g, _, n = scales.shape
    words = np.ascontiguousarray(words).reshape(g, 128, n, -1)
    if fmt == "e4m3":
        vals = words.view(ml_dtypes.float8_e4m3fn).astype(np.float64)
    else:
        nib = np.empty((g, 128, n, 4), np.uint8)
        nib[..., 0::2] = words & 0xF
        nib[..., 1::2] = words >> 4
        vals = E2M1[nib]
    vals = vals * np.repeat(np.exp2(scales.astype(np.float64) - 127.0), 8, axis=1)[..., None]
    return vals.transpose(0, 1, 3, 2).reshape(g * 512, n)


def sigmoid(v):
    return 1.0 / (1.0 + np.exp(-v))


K, T, J, R, N, E = 512, 2048, 256, 512, 256, 1024


def setup_inputs():
    n = np.random.standard_normal
    idx = np.random.permutation(T)[:J]
    idx2 = np.random.permutation(T)[:J]
    idx3 = np.random.permutation(E)[:J]
    fk = mx_kscale(K)
    fr = mx_kscale(R)
    xtp = pack_weight(n((K, T)) / fk[:, None], "e2m1")
    wp = pack_weight(n((K, R)) * 1 / np.sqrt(K) * fk[:, None] * fr, "e4m3")
    wbp = pack_weight(n((R, N)) * 1 / np.sqrt(R) / fr[:, None], "e2m1")
    wsp = pack_weight(n((K, N)) * 1 / np.sqrt(K) * fk[:, None], "e4m3")
    return {
        "xt_words": xtp[0],
        "xt_scales": xtp[1],
        "w_words": wp[0],
        "w_scales": wp[1],
        "wb_words": wbp[0],
        "wb_scales": wbp[1],
        "ws_words": wsp[0],
        "ws_scales": wsp[1],
        "tz": (n((N, E))).astype(np.float32),
        "so": (np.random.uniform(0.6, 1.6, (N, 1))).astype(np.float32),
        "bo": (np.random.uniform(-1.0, 1.0, (N, 1))).astype(np.float32),
        "offs": striped(idx),
        "offs2": striped(idx2),
        "offs3": striped(idx3),
    }


def reference(xt_words, xt_scales, w_words, w_scales, wb_words, wb_scales, ws_words, ws_scales, tz, so, bo, offs, offs2, offs3):
    idx = unstriped(offs)
    idx2 = unstriped(offs2)
    idx3 = unstriped(offs3)
    xtu = unpack_weight(xt_words, xt_scales, "e2m1")
    wu = unpack_weight(w_words, w_scales, "e4m3")
    wbu = unpack_weight(wb_words, wb_scales, "e2m1")
    wsu = unpack_weight(ws_words, ws_scales, "e4m3")
    xtidxg = xtu[:, idx]
    a = wu.T @ xtidxg
    xtidx2g = xtu[:, idx2]
    b = wu.T @ xtidx2g
    hid = np.abs(a - b)
    hidq = mxq(hid, 0, "e5m2")
    p = wbu.T @ hidq + wsu.T @ xtidx2g
    y = p * sigmoid(f64(tz)[:, idx3] * f64(so) + f64(bo))
    return y

@@ -1,0 +1,186 @@
+from contextlib import ExitStack
+
+import concourse.mybir as mybir
+
+K, T, J, R, N, E = 512, 2048, 256, 512, 256, 1024
+FLOPS = 2 * K * R * J * 2 + 2 * R * N * J + 2 * K * N * J
+
+F32 = mybir.dt.float32
+BF16 = mybir.dt.bfloat16
+I32 = mybir.dt.int32
+U32 = mybir.dt.uint32
+U16 = mybir.dt.uint16
+U8 = mybir.dt.uint8
+E4M3 = mybir.dt.float8_e4m3fn_x4
+E5M2 = mybir.dt.float8_e5m2_x4
+E2M1 = mybir.dt.float4_e2m1fn_x4
+ACT = mybir.ActivationFunctionType
+ALU = mybir.AluOpType
+
+P = 128
+PACK = 4
+CHUNK = 128
+HALVES = N // P
+PART = CHUNK // 2
+
+
+def load_scale_rows(queue, plane, rows, quadrants=range(4)):
+    for q in quadrants:
+        queue.dma_start(out=plane[32 * q : 32 * q + 4, :].bitcast(I32), in_=rows[0, 4 * q : 4 * q + 4, :].bitcast(I32))
+
+
+def tile_list_tied_direct_skip_finalgate_kernel(
+    tc, xt_words, xt_scales, w_words, w_scales, wb_words, wb_scales, ws_words, ws_scales, tz, so, bo, offs, offs2, offs3, out
+):
+    nc = tc.nc
+    with ExitStack() as ctx:
+        keep = ctx.enter_context(tc.tile_pool(name="keep", bufs=1))
+        reuse = ctx.enter_context(tc.tile_pool(name="reuse", bufs=1))
+        psum = ctx.enter_context(tc.psum_pool(name="psum", bufs=1))
+
+        list1 = keep.tile([P, J // 16], U16, name="list1")
+        list2 = keep.tile([P, J // 16], U16, name="list2")
+        list3 = keep.tile([P, J // 16], U16, name="list3")
+        x_words = keep.tile([P, T], U16, name="x_words", align_bytes=64)
+        x_plane = keep.tile([P, T], U8, name="x_plane", align_bytes=64)
+        w_raw = keep.tile([P, R], U32, name="w_raw", align_bytes=64)
+        w_raw_plane = reuse.tile([P, R], U8, name="w_raw_plane", align_bytes=64, offset=0)
+        w_codes = keep.tile([P, R], U32, name="w_codes", align_bytes=64)
+        w_plane = keep.tile([P, R], U8, name="w_plane", align_bytes=64)
+        ws_codes = keep.tile([P, N], U32, name="ws_codes", align_bytes=64)
+        ws_plane = keep.tile([P, N], U8, name="ws_plane", align_bytes=64)
+        wb_codes = keep.tile([P, N], U16, name="wb_codes", align_bytes=64)
+        wb_plane = keep.tile([P, N], U8, name="wb_plane", align_bytes=64)
+        tz_rows = [keep.tile([P, E], F32, name="tz_rows%d" % h) for h in range(HALVES)]
+        slope = keep.tile([P, HALVES], F32, name="slope")
+        shift = keep.tile([P, HALVES], F32, name="shift")
+        gate = [keep.tile([P, J], F32, name="gate%d" % h) for h in range(HALVES)]
+        x1_codes = keep.tile([P, J], U16, name="x1_codes", align_bytes=64)
+        x2_codes = reuse.tile([P, J], U16, name="x2_codes", align_bytes=64, offset=J)
+        x1_plane = keep.tile([P, J], U8, name="x1_plane", align_bytes=64)
+        x2_plane = reuse.tile([P, J], U8, name="x2_plane", align_bytes=64, offset=0)
+
+        nc.vector.memset(x_plane[:].bitcast(I32), 0)
+        nc.gpsimd.memset(w_raw_plane[:].bitcast(I32), 0)
+        nc.vector.memset(ws_plane[:].bitcast(I32), 0)
+        nc.vector.memset(wb_plane[:].bitcast(I32), 0)
+        nc.sync.dma_start(list1[:], offs)
+        nc.sync.dma_start(list2[:], offs2)
+        nc.sync.dma_start(out=x_words[:].bitcast(I32), in_=xt_words[0].bitcast(I32))
+        load_scale_rows(nc.sync, x_plane, xt_scales)
+        nc.sync.dma_start(out=w_raw[:].bitcast(I32), in_=w_words[0].rearrange("p c t -> p (c t)").bitcast(I32))
+        load_scale_rows(nc.sync, w_raw_plane, w_scales, range(2))
+        load_scale_rows(nc.gpsimd, w_raw_plane, w_scales, range(2, 4))
+        nc.sync.dma_start(out=tz_rows[0][:], in_=tz[0 * P : 1 * P, :])
+        nc.sync.dma_start(list3[:], offs3)
+        with nc.allow_non_contiguous_dma(reason="one value a partition"):
+            nc.sync.dma_start(out=slope[:], in_=so.rearrange("(h p) o -> p (h o)", p=P))
+        with nc.allow_non_contiguous_dma(reason="one value a partition"):
+            nc.sync.dma_start(out=shift[:], in_=bo.rearrange("(h p) o -> p (h o)", p=P))
+        nc.sync.dma_start(out=ws_codes[:].bitcast(I32), in_=ws_words[0].rearrange("p c t -> p (c t)").bitcast(I32))
+        nc.sync.dma_start(out=tz_rows[1][:], in_=tz[1 * P : 2 * P, :])
+        nc.sync.dma_start(out=wb_codes[:].bitcast(I32), in_=wb_words[0].bitcast(I32))
+        load_scale_rows(nc.sync, wb_plane, wb_scales)
+        load_scale_rows(nc.gpsimd, ws_plane, ws_scales)
+
+        nc.vector.tensor_copy(x1_plane[:], x_plane[:].indirect(list1[:]))
+        nc.vector.tensor_copy(x1_codes[:], x_words[:].indirect(list1[:]))
+        nc.scalar.copy(
+            out=w_codes[:].rearrange("p (t g i) -> p g t i", t=PACK, i=4),
+            in_=w_raw[:].rearrange("p (g i t) -> p g t i", t=PACK, i=4),
+        )
+        for ts in (slice(0, 2), slice(2, 4)):
+            nc.vector.tensor_copy(
+                out=w_plane[:].rearrange("p (t g i) -> p g t i", t=PACK, i=16)[:, :, ts, :],
+                in_=w_raw_plane[:].rearrange("p (g i t) -> p g t i", t=PACK, i=16)[:, :, ts, :],
+            )
+        nc.vector.tensor_copy(x2_plane[:], x_plane[:].indirect(list2[:]))
+        nc.vector.tensor_copy(x2_codes[:], x_words[:].indirect(list2[:]))
+
+        def first_product(bank, codes, plane, cols):
+            for t in range(PACK):
+                rs = slice(t * P, (t + 1) * P)
+                nc.tensor.matmul_mx(
+                    out=bank[:, t * CHUNK : (t + 1) * CHUNK],
+                    lhsT=w_codes[:, rs].bitcast(E4M3),
+                    lhsT_scale=w_plane[:, rs],
+                    rhs=codes[:, cols].bitcast(E2M1),
+                    rhs_scale=plane[:, cols],
+                    start=True,
+                    stop=True,
+                )
+
+        def look_up_gate(h):
+            nc.scalar.activation(
+                out=gate[h][:],
+                in_=tz_rows[h][:].indirect(list3[:]),
+                func=ACT.Sigmoid,
+                bias=shift[:, h : h + 1],
+                scale=slope[:, h : h + 1],
+            )
+
+        chunks = range(J // CHUNK)
+        cols = [slice(c * CHUNK, (c + 1) * CHUNK) for c in chunks]
+        a_bank = [psum.tile([P, PACK * CHUNK], F32, name="a_bank%d" % c) for c in chunks]
+        b_bank = [psum.tile([P, PACK * CHUNK], F32, name="b_bank%d" % c) for c in chunks]
+        p_bank = [[psum.tile([P, CHUNK], F32, name="p_bank%d%d" % (c, h)) for h in range(HALVES)] for c in chunks]
+        a_sb = [keep.tile([P, CHUNK, PACK], F32, name="a_sb%d" % c) for c in chunks]
+
+        for c in chunks:
+            first_product(a_bank[c], x1_codes, x1_plane, cols[c])
+            copy = nc.scalar.copy if c == 0 else nc.vector.tensor_copy
+            copy(out=a_sb[c][:], in_=a_bank[c][:].rearrange("p (t j) -> p j t", t=PACK))
+        for c in chunks:
+            first_product(b_bank[c], x2_codes, x2_plane, cols[c])
+        for c in chunks:
+            for h in range(HALVES):
+                ns = slice(h * P, (h + 1) * P)
+                nc.tensor.matmul_mx(
+                    out=p_bank[c][h][:],
+                    lhsT=ws_codes[:, ns].bitcast(E4M3),
+                    lhsT_scale=ws_plane[:, ns],
+                    rhs=x2_codes[:, cols[c]].bitcast(E2M1),
+                    rhs_scale=x2_plane[:, cols[c]],
+                    start=True,
+                    stop=False,
+                )
+
+        look_up_gate(0)
+        hid = {}
+        for c in chunks:
+            for u in range(CHUNK // PART):
+                js = slice(u * PART, (u + 1) * PART)
+                diff = keep.tile([P, PART, PACK], F32, name="diff%d%d" % (c, u))
+                hid[c, u] = keep.tile([P, PART * PACK], BF16, name="hid%d%d" % (c, u), align_bytes=64)
+                nc.vector.tensor_tensor(
+                    out=diff[:],
+                    in0=b_bank[c][:].rearrange("p (t j) -> p j t", t=PACK)[:, js, :],
+                    in1=a_sb[c][:, js, :],
+                    op=ALU.subtract,
+                )
+                nc.scalar.activation(out=hid[c, u][:], in_=diff[:].rearrange("p j t -> p (j t)"), func=ACT.Abs)
+        look_up_gate(1)
+
+        for c in chunks:
+            hid_codes = keep.tile([P, CHUNK], U32, name="hid_codes%d" % c, align_bytes=64)
+            hid_plane = keep.tile([P, CHUNK], U8, name="hid_plane%d" % c, align_bytes=64)
+            for u in range(CHUNK // PART):
+                js = slice(u * PART, (u + 1) * PART)
+                nc.vector.quantize_mx(out=hid_codes[:, js].bitcast(E5M2), scales=hid_plane[:, js], in_=hid[c, u][:])
+            for h in range(HALVES):
+                ns = slice(h * P, (h + 1) * P)
+                nc.tensor.matmul_mx(
+                    out=p_bank[c][h][:],
+                    lhsT=wb_codes[:, ns].bitcast(E2M1),
+                    lhsT_scale=wb_plane[:, ns],
+                    rhs=hid_codes[:].bitcast(E5M2),
+                    rhs_scale=hid_plane[:],
+                    start=False,
+                    stop=True,
+                )
+        for c in chunks:
+            for h in range(HALVES):
+                result = keep.tile([P, CHUNK], F32, name="result%d%d" % (c, h))
+                nc.vector.tensor_tensor(out=result[:], in0=p_bank[c][h][:], in1=gate[h][:, cols[c]], op=ALU.mult)
+                queue = nc.sync if h == 0 else nc.scalar
+                queue.dma_start(out=out[h * P : (h + 1) * P, cols[c]], in_=result[:])

@@ -61,6 +61,9 @@ def tile_list_tied_direct_skip_finalgate_kernel(
         x2_plane = reuse.tile([P, J], U8, name="x2_plane", align_bytes=64, offset=0)
 
         nc.vector.memset(x_plane[:].bitcast(I32), 0)
+        warm = keep.tile([P, 2], F32, name="warm")
+        nc.vector.memset(warm[:, 0:1], 0.0)
+        nc.scalar.activation(out=warm[:, 1:2], in_=warm[:, 0:1], func=ACT.Sigmoid)
         nc.gpsimd.memset(w_raw_plane[:].bitcast(I32), 0)
         nc.vector.memset(ws_plane[:].bitcast(I32), 0)
         nc.vector.memset(wb_plane[:].bitcast(I32), 0)

@@ -51,14 +51,14 @@ def tile_list_tied_direct_skip_finalgate_kernel(
         ws_plane = keep.tile([P, N], U8, name="ws_plane", align_bytes=64)
         wb_codes = keep.tile([P, N], U16, name="wb_codes", align_bytes=64)
         wb_plane = keep.tile([P, N], U8, name="wb_plane", align_bytes=64)
-        tz_rows = [keep.tile([P, E], F32, name="tz_rows%d" % h) for h in range(HALVES)]
+        tz_rows = [reuse.tile([P, E], F32, name="tz_rows%d" % h, align_bytes=64, offset=R + 4 * E * h) for h in range(HALVES)]
         slope = keep.tile([P, HALVES], F32, name="slope")
         shift = keep.tile([P, HALVES], F32, name="shift")
         gate = [keep.tile([P, J], F32, name="gate%d" % h) for h in range(HALVES)]
         x1_codes = keep.tile([P, J], U16, name="x1_codes", align_bytes=64)
-        x2_codes = reuse.tile([P, J], U16, name="x2_codes", align_bytes=64, offset=J)
+        x2_codes = reuse.tile([P, J], U16, name="x2_codes", align_bytes=64, offset=0)
         x1_plane = keep.tile([P, J], U8, name="x1_plane", align_bytes=64)
-        x2_plane = reuse.tile([P, J], U8, name="x2_plane", align_bytes=64, offset=0)
+        x2_plane = keep.tile([P, J], U8, name="x2_plane", align_bytes=64)
 
         nc.vector.memset(x_plane[:].bitcast(I32), 0)
         warm = keep.tile([P, 2], F32, name="warm")
@@ -81,10 +81,11 @@ def tile_list_tied_direct_skip_finalgate_kernel(
         with nc.allow_non_contiguous_dma(reason="one value a partition"):
             nc.sync.dma_start(out=shift[:], in_=bo.rearrange("(h p) o -> p (h o)", p=P))
         nc.sync.dma_start(out=ws_codes[:].bitcast(I32), in_=ws_words[0].rearrange("p c t -> p (c t)").bitcast(I32))
-        nc.sync.dma_start(out=tz_rows[1][:], in_=tz[1 * P : 2 * P, :])
         nc.sync.dma_start(out=wb_codes[:].bitcast(I32), in_=wb_words[0].bitcast(I32))
+        nc.sync.dma_start(out=tz_rows[1][:], in_=tz[1 * P : 2 * P, :])
+        load_scale_rows(nc.gpsimd, ws_plane, ws_scales, range(1))
+        load_scale_rows(nc.sync, ws_plane, ws_scales, range(1, 4))
         load_scale_rows(nc.sync, wb_plane, wb_scales)
-        load_scale_rows(nc.gpsimd, ws_plane, ws_scales)
 
         nc.vector.tensor_copy(x1_plane[:], x_plane[:].indirect(list1[:]))
         nc.vector.tensor_copy(x1_codes[:], x_words[:].indirect(list1[:]))
@@ -92,12 +93,12 @@ def tile_list_tied_direct_skip_finalgate_kernel(
             out=w_codes[:].rearrange("p (t g i) -> p g t i", t=PACK, i=4),
             in_=w_raw[:].rearrange("p (g i t) -> p g t i", t=PACK, i=4),
         )
+        nc.vector.tensor_copy(x2_plane[:], x_plane[:].indirect(list2[:]))
         for ts in (slice(0, 2), slice(2, 4)):
             nc.vector.tensor_copy(
                 out=w_plane[:].rearrange("p (t g i) -> p g t i", t=PACK, i=16)[:, :, ts, :],
                 in_=w_raw_plane[:].rearrange("p (g i t) -> p g t i", t=PACK, i=16)[:, :, ts, :],
             )
-        nc.vector.tensor_copy(x2_plane[:], x_plane[:].indirect(list2[:]))
         nc.vector.tensor_copy(x2_codes[:], x_words[:].indirect(list2[:]))
 
         def first_product(bank, codes, plane, cols):
@@ -148,42 +149,55 @@ def tile_list_tied_direct_skip_finalgate_kernel(
                     stop=False,
                 )
 
-        look_up_gate(0)
-        hid = {}
-        for c in chunks:
-            for u in range(CHUNK // PART):
-                js = slice(u * PART, (u + 1) * PART)
-                diff = keep.tile([P, PART, PACK], F32, name="diff%d%d" % (c, u))
-                hid[c, u] = keep.tile([P, PART * PACK], BF16, name="hid%d%d" % (c, u), align_bytes=64)
-                nc.vector.tensor_tensor(
-                    out=diff[:],
-                    in0=b_bank[c][:].rearrange("p (t j) -> p j t", t=PACK)[:, js, :],
-                    in1=a_sb[c][:, js, :],
-                    op=ALU.subtract,
-                )
-                nc.scalar.activation(out=hid[c, u][:], in_=diff[:].rearrange("p j t -> p (j t)"), func=ACT.Abs)
-        look_up_gate(1)
+        def difference(c, u):
+            js = slice(u * PART, (u + 1) * PART)
+            diff = keep.tile([P, PART, PACK], F32, name="diff%d%d" % (c, u))
+            nc.vector.tensor_tensor(
+                out=diff[:],
+                in0=b_bank[c][:].rearrange("p (t j) -> p j t", t=PACK)[:, js, :],
+                in1=a_sb[c][:, js, :],
+                op=ALU.subtract,
+            )
+            return diff[:].rearrange("p j t -> p (j t)")
 
-        for c in chunks:
-            hid_codes = keep.tile([P, CHUNK], U32, name="hid_codes%d" % c, align_bytes=64)
-            hid_plane = keep.tile([P, CHUNK], U8, name="hid_plane%d" % c, align_bytes=64)
-            for u in range(CHUNK // PART):
-                js = slice(u * PART, (u + 1) * PART)
-                nc.vector.quantize_mx(out=hid_codes[:, js].bitcast(E5M2), scales=hid_plane[:, js], in_=hid[c, u][:])
+        def second_product(c):
             for h in range(HALVES):
                 ns = slice(h * P, (h + 1) * P)
                 nc.tensor.matmul_mx(
                     out=p_bank[c][h][:],
                     lhsT=wb_codes[:, ns].bitcast(E2M1),
                     lhsT_scale=wb_plane[:, ns],
-                    rhs=hid_codes[:].bitcast(E5M2),
-                    rhs_scale=hid_plane[:],
+                    rhs=hid_codes[c][:].bitcast(E5M2),
+                    rhs_scale=hid_plane[c][:],
                     start=False,
                     stop=True,
                 )
+
+        hid_codes = [keep.tile([P, CHUNK], U32, name="hid_codes%d" % c, align_bytes=64) for c in chunks]
+        hid_plane = [keep.tile([P, CHUNK], U8, name="hid_plane%d" % c, align_bytes=64) for c in chunks]
+        width = PART * PACK
+
+        look_up_gate(0)
+        hid0 = reuse.tile([P, 2 * width], BF16, name="hid0", align_bytes=64, offset=R)
+        for u in range(2):
+            nc.scalar.activation(out=hid0[:, u * width : (u + 1) * width], in_=difference(0, u), func=ACT.Abs)
+        nc.vector.quantize_mx(out=hid_codes[0][:].bitcast(E5M2), scales=hid_plane[0][:], in_=hid0[:])
+        second_product(0)
+
+        hid1a = reuse.tile([P, width], BF16, name="hid1a", align_bytes=64, offset=R + 4 * width)
+        hid1b = reuse.tile([P, width], BF16, name="hid1b", align_bytes=64, offset=R)
+        nc.scalar.activation(out=hid1a[:], in_=difference(1, 0), func=ACT.Abs)
+        last = difference(1, 1)
+        nc.vector.scalar_tensor_tensor(out=hid1b[:], in0=last, scalar=-1.0, in1=last, op0=ALU.mult, op1=ALU.max)
+        for u, hid in enumerate((hid1a, hid1b)):
+            js = slice(u * PART, (u + 1) * PART)
+            nc.vector.quantize_mx(out=hid_codes[1][:, js].bitcast(E5M2), scales=hid_plane[1][:, js], in_=hid[:])
+        second_product(1)
+
+        look_up_gate(1)
         for c in chunks:
             for h in range(HALVES):
                 result = keep.tile([P, CHUNK], F32, name="result%d%d" % (c, h))
                 nc.vector.tensor_tensor(out=result[:], in0=p_bank[c][h][:], in1=gate[h][:, cols[c]], op=ALU.mult)
-                queue = nc.sync if h == 0 else nc.scalar
+                queue = nc.scalar if h == 0 else nc.sync
                 queue.dma_start(out=out[h * P : (h + 1) * P, cols[c]], in_=result[:])

@@ -52,8 +52,8 @@ def tile_list_tied_direct_skip_finalgate_kernel(
         wb_codes = keep.tile([P, N], U16, name="wb_codes", align_bytes=64)
         wb_plane = keep.tile([P, N], U8, name="wb_plane", align_bytes=64)
         tz_rows = [reuse.tile([P, E], F32, name="tz_rows%d" % h, align_bytes=64, offset=R + 4 * E * h) for h in range(HALVES)]
-        slope = keep.tile([P, HALVES], F32, name="slope")
-        shift = keep.tile([P, HALVES], F32, name="shift")
+        slope = keep.tile([P, HALVES, 8], F32, name="slope")
+        shift = keep.tile([P, HALVES, 8], F32, name="shift")
         gate = [keep.tile([P, J], F32, name="gate%d" % h) for h in range(HALVES)]
         x1_codes = keep.tile([P, J], U16, name="x1_codes", align_bytes=64)
         x2_codes = reuse.tile([P, J], U16, name="x2_codes", align_bytes=64, offset=0)
@@ -69,31 +69,30 @@ def tile_list_tied_direct_skip_finalgate_kernel(
         nc.vector.memset(wb_plane[:].bitcast(I32), 0)
         nc.sync.dma_start(list1[:], offs)
         nc.sync.dma_start(list2[:], offs2)
-        nc.sync.dma_start(out=x_words[:].bitcast(I32), in_=xt_words[0].bitcast(I32))
-        load_scale_rows(nc.sync, x_plane, xt_scales)
         nc.sync.dma_start(out=w_raw[:].bitcast(I32), in_=w_words[0].rearrange("p c t -> p (c t)").bitcast(I32))
-        load_scale_rows(nc.sync, w_raw_plane, w_scales, range(2))
-        load_scale_rows(nc.gpsimd, w_raw_plane, w_scales, range(2, 4))
+        load_scale_rows(nc.sync, x_plane, xt_scales)
+        nc.sync.dma_start(out=x_words[:].bitcast(I32), in_=xt_words[0].bitcast(I32))
+        load_scale_rows(nc.sync, w_raw_plane, w_scales, range(3))
+        load_scale_rows(nc.gpsimd, w_raw_plane, w_scales, range(3, 4))
         nc.sync.dma_start(out=tz_rows[0][:], in_=tz[0 * P : 1 * P, :])
         nc.sync.dma_start(list3[:], offs3)
         with nc.allow_non_contiguous_dma(reason="one value a partition"):
-            nc.sync.dma_start(out=slope[:], in_=so.rearrange("(h p) o -> p (h o)", p=P))
-        with nc.allow_non_contiguous_dma(reason="one value a partition"):
-            nc.sync.dma_start(out=shift[:], in_=bo.rearrange("(h p) o -> p (h o)", p=P))
+            nc.sync.dma_start(out=slope[:, :, 0:1], in_=so.rearrange("(h p) o -> p h o", p=P))
+            nc.sync.dma_start(out=shift[:, :, 0:1], in_=bo.rearrange("(h p) o -> p h o", p=P))
         nc.sync.dma_start(out=ws_codes[:].bitcast(I32), in_=ws_words[0].rearrange("p c t -> p (c t)").bitcast(I32))
         nc.sync.dma_start(out=wb_codes[:].bitcast(I32), in_=wb_words[0].bitcast(I32))
         nc.sync.dma_start(out=tz_rows[1][:], in_=tz[1 * P : 2 * P, :])
-        load_scale_rows(nc.gpsimd, ws_plane, ws_scales, range(1))
-        load_scale_rows(nc.sync, ws_plane, ws_scales, range(1, 4))
+        load_scale_rows(nc.gpsimd, ws_plane, ws_scales, range(2))
+        load_scale_rows(nc.sync, ws_plane, ws_scales, range(2, 4))
         load_scale_rows(nc.sync, wb_plane, wb_scales)
 
         nc.vector.tensor_copy(x1_plane[:], x_plane[:].indirect(list1[:]))
+        nc.vector.tensor_copy(x2_plane[:], x_plane[:].indirect(list2[:]))
         nc.vector.tensor_copy(x1_codes[:], x_words[:].indirect(list1[:]))
         nc.scalar.copy(
             out=w_codes[:].rearrange("p (t g i) -> p g t i", t=PACK, i=4),
             in_=w_raw[:].rearrange("p (g i t) -> p g t i", t=PACK, i=4),
         )
-        nc.vector.tensor_copy(x2_plane[:], x_plane[:].indirect(list2[:]))
         for ts in (slice(0, 2), slice(2, 4)):
             nc.vector.tensor_copy(
                 out=w_plane[:].rearrange("p (t g i) -> p g t i", t=PACK, i=16)[:, :, ts, :],
@@ -119,8 +118,8 @@ def tile_list_tied_direct_skip_finalgate_kernel(
                 out=gate[h][:],
                 in_=tz_rows[h][:].indirect(list3[:]),
                 func=ACT.Sigmoid,
-                bias=shift[:, h : h + 1],
-                scale=slope[:, h : h + 1],
+                bias=shift[:, h, 0:1],
+                scale=slope[:, h, 0:1],
             )
 
         chunks = range(J // CHUNK)
@@ -128,11 +127,14 @@ def tile_list_tied_direct_skip_finalgate_kernel(
         a_bank = [psum.tile([P, PACK * CHUNK], F32, name="a_bank%d" % c) for c in chunks]
         b_bank = [psum.tile([P, PACK * CHUNK], F32, name="b_bank%d" % c) for c in chunks]
         p_bank = [[psum.tile([P, CHUNK], F32, name="p_bank%d%d" % (c, h)) for h in range(HALVES)] for c in chunks]
-        a_sb = [keep.tile([P, CHUNK, PACK], F32, name="a_sb%d" % c) for c in chunks]
+        a_sb = [
+            keep.tile([P, CHUNK, PACK], F32, name="a_sb0"),
+            reuse.tile([P, CHUNK, PACK], F32, name="a_sb1", align_bytes=64, offset=R + 2 * E),
+        ]
 
         for c in chunks:
             first_product(a_bank[c], x1_codes, x1_plane, cols[c])
-            copy = nc.scalar.copy if c == 0 else nc.vector.tensor_copy
+            copy = nc.vector.tensor_copy if c == 0 else nc.scalar.copy
             copy(out=a_sb[c][:], in_=a_bank[c][:].rearrange("p (t j) -> p j t", t=PACK))
         for c in chunks:
             first_product(b_bank[c], x2_codes, x2_plane, cols[c])

from contextlib import ExitStack

import concourse.mybir as mybir

K, T, J, R, N, E = 512, 2048, 256, 512, 256, 1024
FLOPS = 2 * K * R * J * 2 + 2 * R * N * J + 2 * K * N * J

F32 = mybir.dt.float32
BF16 = mybir.dt.bfloat16
I32 = mybir.dt.int32
U32 = mybir.dt.uint32
U16 = mybir.dt.uint16
U8 = mybir.dt.uint8
E4M3 = mybir.dt.float8_e4m3fn_x4
E5M2 = mybir.dt.float8_e5m2_x4
E2M1 = mybir.dt.float4_e2m1fn_x4
ACT = mybir.ActivationFunctionType
ALU = mybir.AluOpType

P = 128
PACK = 4
CHUNK = 128
HALVES = N // P
PART = CHUNK // 2


def load_scale_rows(queue, plane, rows, quadrants=range(4)):
    for q in quadrants:
        queue.dma_start(out=plane[32 * q : 32 * q + 4, :].bitcast(I32), in_=rows[0, 4 * q : 4 * q + 4, :].bitcast(I32))


def tile_list_tied_direct_skip_finalgate_kernel(
    tc, xt_words, xt_scales, w_words, w_scales, wb_words, wb_scales, ws_words, ws_scales, tz, so, bo, offs, offs2, offs3, out
):
    nc = tc.nc
    with ExitStack() as ctx:
        keep = ctx.enter_context(tc.tile_pool(name="keep", bufs=1))
        reuse = ctx.enter_context(tc.tile_pool(name="reuse", bufs=1))
        psum = ctx.enter_context(tc.psum_pool(name="psum", bufs=1))

        list1 = keep.tile([P, J // 16], U16, name="list1")
        list2 = keep.tile([P, J // 16], U16, name="list2")
        list3 = keep.tile([P, J // 16], U16, name="list3")
        x_words = keep.tile([P, T], U16, name="x_words", align_bytes=64)
        x_plane = keep.tile([P, T], U8, name="x_plane", align_bytes=64)
        w_raw = keep.tile([P, R], U32, name="w_raw", align_bytes=64)
        w_raw_plane = reuse.tile([P, R], U8, name="w_raw_plane", align_bytes=64, offset=0)
        w_codes = keep.tile([P, R], U32, name="w_codes", align_bytes=64)
        w_plane = keep.tile([P, R], U8, name="w_plane", align_bytes=64)
        ws_codes = keep.tile([P, N], U32, name="ws_codes", align_bytes=64)
        ws_plane = keep.tile([P, N], U8, name="ws_plane", align_bytes=64)
        wb_codes = keep.tile([P, N], U16, name="wb_codes", align_bytes=64)
        wb_plane = keep.tile([P, N], U8, name="wb_plane", align_bytes=64)
        tz_rows = [reuse.tile([P, E], F32, name="tz_rows%d" % h, align_bytes=64, offset=R + 4 * E * h) for h in range(HALVES)]
        slope = keep.tile([P, HALVES, 8], F32, name="slope")
        shift = keep.tile([P, HALVES, 8], F32, name="shift")
        gate = [keep.tile([P, J], F32, name="gate%d" % h) for h in range(HALVES)]
        x1_codes = keep.tile([P, J], U16, name="x1_codes", align_bytes=64)
        x2_codes = reuse.tile([P, J], U16, name="x2_codes", align_bytes=64, offset=0)
        x1_plane = keep.tile([P, J], U8, name="x1_plane", align_bytes=64)
        x2_plane = keep.tile([P, J], U8, name="x2_plane", align_bytes=64)

        nc.vector.memset(x_plane[:].bitcast(I32), 0)
        warm = keep.tile([P, 2], F32, name="warm")
        nc.vector.memset(warm[:, 0:1], 0.0)
        nc.scalar.activation(out=warm[:, 1:2], in_=warm[:, 0:1], func=ACT.Sigmoid)
        nc.gpsimd.memset(w_raw_plane[:].bitcast(I32), 0)
        nc.vector.memset(ws_plane[:].bitcast(I32), 0)
        nc.vector.memset(wb_plane[:].bitcast(I32), 0)
        nc.sync.dma_start(list1[:], offs)
        nc.sync.dma_start(list2[:], offs2)
        nc.sync.dma_start(out=w_raw[:].bitcast(I32), in_=w_words[0].rearrange("p c t -> p (c t)").bitcast(I32))
        load_scale_rows(nc.sync, x_plane, xt_scales)
        nc.sync.dma_start(out=x_words[:].bitcast(I32), in_=xt_words[0].bitcast(I32))
        load_scale_rows(nc.sync, w_raw_plane, w_scales, range(3))
        load_scale_rows(nc.gpsimd, w_raw_plane, w_scales, range(3, 4))
        nc.sync.dma_start(out=tz_rows[0][:], in_=tz[0 * P : 1 * P, :])
        nc.sync.dma_start(list3[:], offs3)
        with nc.allow_non_contiguous_dma(reason="one value a partition"):
            nc.sync.dma_start(out=slope[:, :, 0:1], in_=so.rearrange("(h p) o -> p h o", p=P))
            nc.sync.dma_start(out=shift[:, :, 0:1], in_=bo.rearrange("(h p) o -> p h o", p=P))
        nc.sync.dma_start(out=ws_codes[:].bitcast(I32), in_=ws_words[0].rearrange("p c t -> p (c t)").bitcast(I32))
        nc.sync.dma_start(out=wb_codes[:].bitcast(I32), in_=wb_words[0].bitcast(I32))
        nc.sync.dma_start(out=tz_rows[1][:], in_=tz[1 * P : 2 * P, :])
        load_scale_rows(nc.gpsimd, ws_plane, ws_scales, range(2))
        load_scale_rows(nc.sync, ws_plane, ws_scales, range(2, 4))
        load_scale_rows(nc.sync, wb_plane, wb_scales)

        nc.vector.tensor_copy(x1_plane[:], x_plane[:].indirect(list1[:]))
        nc.vector.tensor_copy(x2_plane[:], x_plane[:].indirect(list2[:]))
        nc.vector.tensor_copy(x1_codes[:], x_words[:].indirect(list1[:]))
        nc.scalar.copy(
            out=w_codes[:].rearrange("p (t g i) -> p g t i", t=PACK, i=4),
            in_=w_raw[:].rearrange("p (g i t) -> p g t i", t=PACK, i=4),
        )
        for ts in (slice(0, 2), slice(2, 4)):
            nc.vector.tensor_copy(
                out=w_plane[:].rearrange("p (t g i) -> p g t i", t=PACK, i=16)[:, :, ts, :],
                in_=w_raw_plane[:].rearrange("p (g i t) -> p g t i", t=PACK, i=16)[:, :, ts, :],
            )
        nc.vector.tensor_copy(x2_codes[:], x_words[:].indirect(list2[:]))

        def first_product(bank, codes, plane, cols):
            for t in range(PACK):
                rs = slice(t * P, (t + 1) * P)
                nc.tensor.matmul_mx(
                    out=bank[:, t * CHUNK : (t + 1) * CHUNK],
                    lhsT=w_codes[:, rs].bitcast(E4M3),
                    lhsT_scale=w_plane[:, rs],
                    rhs=codes[:, cols].bitcast(E2M1),
                    rhs_scale=plane[:, cols],
                    start=True,
                    stop=True,
                )

        def look_up_gate(h):
            nc.scalar.activation(
                out=gate[h][:],
                in_=tz_rows[h][:].indirect(list3[:]),
                func=ACT.Sigmoid,
                bias=shift[:, h, 0:1],
                scale=slope[:, h, 0:1],
            )

        chunks = range(J // CHUNK)
        cols = [slice(c * CHUNK, (c + 1) * CHUNK) for c in chunks]
        a_bank = [psum.tile([P, PACK * CHUNK], F32, name="a_bank%d" % c) for c in chunks]
        b_bank = [psum.tile([P, PACK * CHUNK], F32, name="b_bank%d" % c) for c in chunks]
        p_bank = [[psum.tile([P, CHUNK], F32, name="p_bank%d%d" % (c, h)) for h in range(HALVES)] for c in chunks]
        a_sb = [
            keep.tile([P, CHUNK, PACK], F32, name="a_sb0"),
            reuse.tile([P, CHUNK, PACK], F32, name="a_sb1", align_bytes=64, offset=R + 2 * E),
        ]

        for c in chunks:
            first_product(a_bank[c], x1_codes, x1_plane, cols[c])
            copy = nc.vector.tensor_copy if c == 0 else nc.scalar.copy
            copy(out=a_sb[c][:], in_=a_bank[c][:].rearrange("p (t j) -> p j t", t=PACK))
        for c in chunks:
            first_product(b_bank[c], x2_codes, x2_plane, cols[c])
        for c in chunks:
            for h in range(HALVES):
                ns = slice(h * P, (h + 1) * P)
                nc.tensor.matmul_mx(
                    out=p_bank[c][h][:],
                    lhsT=ws_codes[:, ns].bitcast(E4M3),
                    lhsT_scale=ws_plane[:, ns],
                    rhs=x2_codes[:, cols[c]].bitcast(E2M1),
                    rhs_scale=x2_plane[:, cols[c]],
                    start=True,
                    stop=False,
                )

        def difference(c, u):
            js = slice(u * PART, (u + 1) * PART)
            diff = keep.tile([P, PART, PACK], F32, name="diff%d%d" % (c, u))
            nc.vector.tensor_tensor(
                out=diff[:],
                in0=b_bank[c][:].rearrange("p (t j) -> p j t", t=PACK)[:, js, :],
                in1=a_sb[c][:, js, :],
                op=ALU.subtract,
            )
            return diff[:].rearrange("p j t -> p (j t)")

        def second_product(c):
            for h in range(HALVES):
                ns = slice(h * P, (h + 1) * P)
                nc.tensor.matmul_mx(
                    out=p_bank[c][h][:],
                    lhsT=wb_codes[:, ns].bitcast(E2M1),
                    lhsT_scale=wb_plane[:, ns],
                    rhs=hid_codes[c][:].bitcast(E5M2),
                    rhs_scale=hid_plane[c][:],
                    start=False,
                    stop=True,
                )

        hid_codes = [keep.tile([P, CHUNK], U32, name="hid_codes%d" % c, align_bytes=64) for c in chunks]
        hid_plane = [keep.tile([P, CHUNK], U8, name="hid_plane%d" % c, align_bytes=64) for c in chunks]
        width = PART * PACK

        look_up_gate(0)
        hid0 = reuse.tile([P, 2 * width], BF16, name="hid0", align_bytes=64, offset=R)
        for u in range(2):
            nc.scalar.activation(out=hid0[:, u * width : (u + 1) * width], in_=difference(0, u), func=ACT.Abs)
        nc.vector.quantize_mx(out=hid_codes[0][:].bitcast(E5M2), scales=hid_plane[0][:], in_=hid0[:])
        second_product(0)

        hid1a = reuse.tile([P, width], BF16, name="hid1a", align_bytes=64, offset=R + 4 * width)
        hid1b = reuse.tile([P, width], BF16, name="hid1b", align_bytes=64, offset=R)
        nc.scalar.activation(out=hid1a[:], in_=difference(1, 0), func=ACT.Abs)
        last = difference(1, 1)
        nc.vector.scalar_tensor_tensor(out=hid1b[:], in0=last, scalar=-1.0, in1=last, op0=ALU.mult, op1=ALU.max)
        for u, hid in enumerate((hid1a, hid1b)):
            js = slice(u * PART, (u + 1) * PART)
            nc.vector.quantize_mx(out=hid_codes[1][:, js].bitcast(E5M2), scales=hid_plane[1][:, js], in_=hid[:])
        second_product(1)

        look_up_gate(1)
        for c in chunks:
            for h in range(HALVES):
                result = keep.tile([P, CHUNK], F32, name="result%d%d" % (c, h))
                nc.vector.tensor_tensor(out=result[:], in0=p_bank[c][h][:], in1=gate[h][:, cols[c]], op=ALU.mult)
                queue = nc.scalar if h == 0 else nc.sync
                queue.dma_start(out=out[h * P : (h + 1) * P, cols[c]], in_=result[:])
